import numpy as np
import ml_dtypes


def mxq(x, axis, fmt="e4m3"):
    dtype, down = {"e4m3": (ml_dtypes.float8_e4m3fn, 7), "e5m2": (ml_dtypes.float8_e5m2, 14)}[fmt]
    v = np.moveaxis(np.asarray(x, np.float32).astype(ml_dtypes.bfloat16).astype(np.float64), axis, -1)
    blocks = v.reshape(v.shape[:-1] + (-1, 32))
    amax = np.abs(blocks).max(-1, keepdims=True)
    byte = np.maximum(np.where(amax > 0, np.frexp(amax)[1] - 1 + 127, 0) - down, 1)
    scale = np.exp2(byte - 127.0)
    codes = (blocks / scale).astype(np.float32).astype(dtype).astype(np.float64)
    return np.moveaxis((codes * scale).reshape(v.shape), -1, axis)


WIDE = False


def mx_kscale(k):
    if not WIDE:
        return np.ones(k)
    levels = np.array([10, -10, 5, -5, 0])
    if k % 512:
        return np.exp2(np.random.permutation(np.resize(levels, k // 32))).repeat(32)
    a = np.empty((k // 512, 16))
    for p in range(k // 512):
        a[p, :8] = np.random.permutation(np.resize(levels, 8))
        for g in range(8):
            far = levels[np.abs(levels - a[p, g]) >= 10]
            a[p, g + 8] = far[np.random.randint(len(far))]
    return np.exp2(a.ravel()).repeat(32)


def f64(x):
    return np.asarray(x).astype(np.float64)


def striped(idx):
    return np.tile(idx.reshape(-1, 16).T, (8, 1)).astype(np.uint16)


def unstriped(offs):
    return offs[:16].T.reshape(-1).astype(np.int64)


def pack_weight(w):
    k, n = w.shape
    w = f64(np.asarray(w, np.float32).astype(ml_dtypes.bfloat16)).reshape(k // 32, 32, n)
    amax = np.abs(w).max(1)
    byte = np.clip(np.where(amax > 0, np.frexp(amax)[1] - 1 + 127 - 7, 1), 1, 254)
    scaled = (w * np.exp2(127.0 - byte)[:, None, :]).reshape(k, n).astype(np.float32)
    words = np.ascontiguousarray(scaled.reshape(k // 512, 128, 4, n).transpose(0, 1, 3, 2)).astype(ml_dtypes.float8_e4m3fn).view(np.uint8)
    return words, np.ascontiguousarray(byte.astype(np.uint8).reshape(k // 512, 16, n))


def unpack_weight(words, scales):
    g, p, n, _ = words.shape
    vals = np.ascontiguousarray(words).view(ml_dtypes.float8_e4m3fn).astype(np.float64) * np.repeat(np.exp2(scales.astype(np.float64) - 127.0), 8, axis=1)[..., None]
    return vals.transpose(0, 1, 3, 2).reshape(g * 512, n)


def planes(y):
    n, m = y.shape
    v = y.astype(np.float32).astype(ml_dtypes.bfloat16).astype(np.float64).reshape(n // 32, 32, m)
    top = np.abs(v).max(1)
    byte = np.clip(np.where(top > 0, np.frexp(top)[1] - 1 + 127 - 7, 1), 1, 254)
    codes = (v * np.exp2(127.0 - byte)[:, None, :]).reshape(n, m).astype(np.float32).astype(ml_dtypes.float8_e4m3fn).view(np.uint8)
    words = codes.reshape(n // 512, 128, 4, m).transpose(0, 1, 3, 2)
    return np.ascontiguousarray(words), np.ascontiguousarray(byte.astype(np.uint8).reshape(n // 512, 16, m))


def sigmoid(v):
    return 1.0 / (1.0 + np.exp(-np.maximum(v, -700.0)))


K, T, S, H, N = 512, 2048, 512, 512, 512


def setup_inputs():
    n = np.random.standard_normal
    s = mx_kscale(K)[:, None]
    u = mx_kscale(H)
    packed_xT = pack_weight(n((K, T)) * s)
    return {
        "x_words": packed_xT[0],
        "x_scales": packed_xT[1],
        "w1": (n((K, H)) / np.sqrt(2 * K) / s * u).astype(np.float32),
        "w2": (n((K, H)) / np.sqrt(2 * K) / s * u).astype(np.float32),
        "w3": (n((H, N)) / np.sqrt(H) / u[:, None]).astype(np.float32),
        "w4": (n((K, N)) / np.sqrt(K) / s).astype(np.float32),
        "offs": striped(np.random.permutation(T)[:S]),
        "dst": striped(np.random.permutation(T)[:S]),
    }


def reference(x_words, x_scales, w1, w2, w3, w4, offs, dst):
    xq = unpack_weight(x_words, x_scales)[:, unstriped(offs)]
    x_dst = unpack_weight(x_words, x_scales)[:, unstriped(dst)]
    y = mxq(f64(w1), 0, "e4m3").T @ xq + mxq(f64(w2), 0, "e4m3").T @ x_dst
    h = np.maximum(y, 0.2 * y)
    e = sigmoid(mxq(f64(w3), 0, "e4m3").T @ mxq(h, 0, "e4m3"))
    v = mxq(f64(w4), 0, "e4m3").T @ xq
    out_0 = e * v
    return (out_0,) + planes(out_0)

@@ -1,0 +1,212 @@
+from contextlib import ExitStack
+
+import concourse.mybir as mybir
+
+F32 = mybir.dt.float32
+BF16 = mybir.dt.bfloat16
+I32 = mybir.dt.int32
+U32 = mybir.dt.uint32
+U16 = mybir.dt.uint16
+U8 = mybir.dt.uint8
+FP8X4 = mybir.dt.float8_e4m3fn_x4
+ACT = mybir.ActivationFunctionType
+ALU = mybir.AluOpType
+
+P = 128
+K = 512
+T = 2048
+S = 512
+CH = 128
+NCH = S // CH
+FLOPS = 4 * 2 * 512 * 512 * 512
+
+
+def tile_picked_zgatt_sigmoid_po_kernel(tc, x_words, x_scales, w1, w2, w3, w4, offs, dst, out_0, out_1, out_2):
+    nc = tc.nc
+    with ExitStack() as ctx:
+        keep = ctx.enter_context(tc.tile_pool(name="keep", bufs=1))
+        psum = ctx.enter_context(tc.psum_pool(name="psum", bufs=1))
+
+        offs_t = keep.tile([P, S // 16], U16, name="offs_t")
+        dst_t = keep.tile([P, S // 16], U16, name="dst_t")
+        xw = keep.tile([P, T], I32, name="xw", align_bytes=64)
+        xs = keep.tile([P, T], U8, name="xs", align_bytes=64)
+        warm = keep.tile([P, 8], F32, name="warm")
+        warm2 = keep.tile([P, 8], F32, name="warm2")
+
+        nc.vector.memset(xs[:].bitcast(I32), 0)
+        nc.vector.memset(warm[:], 0.0)
+        nc.sync.dma_start(offs_t[:], offs)
+        nc.sync.dma_start(dst_t[:], dst)
+        xw_hbm = x_words[0].rearrange("p n t -> p (n t)").bitcast(I32)
+        nc.sync.dma_start(xw[:, 0:512], xw_hbm[:, 0:512])
+        for q in range(4):
+            nc.sync.dma_start(xs[32 * q : 32 * q + 4, :].bitcast(I32), x_scales[0, 4 * q : 4 * q + 4, :].bitcast(I32))
+        nc.sync.dma_start(xw[:, 512:T], xw_hbm[:, 512:T])
+        nc.scalar.activation(warm2[:], warm[:], ACT.Sigmoid)
+        raw = {}
+        for name, w in (("w1", w1), ("w2", w2), ("w3", w3), ("w4", w4)):
+            raw[name] = keep.tile([P, 4, K], F32, name="raw_" + name, align_bytes=64)
+            nc.sync.dma_start(raw[name][:], w.rearrange("(p j) c -> p j c", j=4))
+
+        gw, gs = {}, {}
+        for name, lst in (("offs", offs_t), ("dst", dst_t)):
+            gs[name] = keep.tile([P, S], U8, name="gs_" + name, align_bytes=64)
+            nc.vector.tensor_copy(gs[name][:], xs[:].indirect(lst[:]))
+        for name, lst in (("offs", offs_t), ("dst", dst_t)):
+            gw[name] = keep.tile([P, S], U32, name="gw_" + name, align_bytes=64)
+            nc.vector.tensor_copy(gw[name][:], xw[:].bitcast(U32).indirect(lst[:]))
+
+        grouped, codes, scales = {}, {}, {}
+        clk = keep.tile([P, 64], F32, name="clk")
+
+        def copy_on(eng, out, in_):
+            if eng == "V":
+                nc.vector.tensor_copy(out, in_)
+            elif eng == "S":
+                nc.scalar.copy(out, in_)
+            else:
+                nc.gpsimd.tensor_scalar(out, in_, 1.0, 0.0, ALU.mult, ALU.add)
+
+        def cast_w(name, u, eng):
+            g = keep.tile([P, 2, P, 4], BF16, name="grp_%s_%d" % (name, u), align_bytes=64)
+            grouped[name, u] = g
+            src = raw[name][:].rearrange("p j (m t) -> p m j t", t=4)[:, :, :, 2 * u : 2 * u + 2]
+            copy_on(eng, g[:].rearrange("p t m j -> p m j t"), src)
+
+        def quant_w(name, u):
+            codes[name, u] = keep.tile([P, 2 * P], U32, name="codes_%s_%d" % (name, u), align_bytes=64)
+            scales[name, u] = keep.tile([P, 2 * P], U8, name="scales_%s_%d" % (name, u), align_bytes=64)
+            nc.vector.quantize_mx(out=codes[name, u][:].bitcast(FP8X4), scales=scales[name, u][:],
+                                  in_=grouped[name, u][:].rearrange("p t m j -> p (t m j)"))
+
+        def mm(bank, t, name, rw, rs, start, stop):
+            cols = slice((t % 2) * P, (t % 2 + 1) * P)
+            nc.tensor.matmul_mx(out=bank[:, t, :], lhsT=codes[name, t // 2][:, cols].bitcast(FP8X4),
+                                lhsT_scale=scales[name, t // 2][:, cols],
+                                rhs=rw.bitcast(FP8X4), rhs_scale=rs, start=start, stop=stop)
+
+        hq, hs, hb, yb, ya, eb, es, vb, of, ob = {}, {}, {}, {}, {}, {}, {}, {}, {}, {}
+
+        def mm_y(c):
+            cols = slice(c * CH, (c + 1) * CH)
+            yb[c] = psum.tile([P, 4, CH], F32, name="ybank%d" % c, tag="a%d" % c)
+            for t in range(4):
+                mm(yb[c], t, "w1", gw["offs"][:, cols], gs["offs"][:, cols], True, False)
+                mm(yb[c], t, "w2", gw["dst"][:, cols], gs["dst"][:, cols], False, True)
+
+        def fifth(c):
+            ya[c] = keep.tile([P, CH, 4], F32, name="a%d" % c)
+            nc.scalar.activation(ya[c][:], yb[c][:].rearrange("p t j -> p j t"), ACT.Copy, scale=0.2)
+
+        def leaky(c):
+            hb[c] = keep.tile([P, CH, 4], BF16, name="hb%d" % c, align_bytes=64)
+            nc.vector.tensor_tensor(hb[c][:], yb[c][:].rearrange("p t j -> p j t"), ya[c][:], ALU.max)
+
+        def quant_h(c):
+            hq[c] = keep.tile([P, CH], U32, name="hq%d" % c, align_bytes=64)
+            hs[c] = keep.tile([P, CH], U8, name="hs%d" % c, align_bytes=64)
+            nc.vector.quantize_mx(out=hq[c][:].bitcast(FP8X4), scales=hs[c][:], in_=hb[c][:].rearrange("p j t -> p (j t)"))
+
+        def mm_e(c):
+            eb[c] = psum.tile([P, 4, CH], F32, name="ebank%d" % c, tag="b%d" % c)
+            for t in range(4):
+                mm(eb[c], t, "w3", hq[c][:], hs[c][:], True, True)
+
+        def sig(c):
+            es[c] = keep.tile([P, 4, CH], F32, name="es%d" % c)
+            nc.scalar.activation(es[c][:], eb[c][:], ACT.Sigmoid)
+
+        ow = keep.tile([P, S], U32, name="ow", align_bytes=64)
+        osc = keep.tile([P, S], U8, name="osc", align_bytes=64)
+        out_v = out_0.rearrange("(p t) j -> p t j", t=4)
+        out_w = out_1[0].rearrange("p n t -> p (n t)").bitcast(I32)
+
+        def mm_v(c):
+            cols = slice(c * CH, (c + 1) * CH)
+            vb[c] = psum.tile([P, 4, CH], F32, name="vbank%d" % c, tag="a%d" % c)
+            for t in range(4):
+                mm(vb[c], t, "w4", gw["offs"][:, cols], gs["offs"][:, cols], True, True)
+
+        def mul(c):
+            cols = slice(c * CH, (c + 1) * CH)
+            of[c] = keep.tile([P, 4, CH], F32, name="o%d" % c)
+            nc.vector.tensor_tensor(of[c][:], vb[c][:], es[c][:], ALU.mult)
+            nc.sync.dma_start(out_v[:, :, cols], of[c][:])
+
+        def cast_o(c, eng):
+            ob[c] = keep.tile([P, CH, 4], BF16, name="ob%d" % c, align_bytes=64)
+            copy_on(eng, ob[c][:].rearrange("p (c i) t -> p c t i", i=4), of[c][:].rearrange("p t (c i) -> p c t i", i=4))
+
+        def quant_o(c):
+            cols = slice(c * CH, (c + 1) * CH)
+            nc.vector.quantize_mx(out=ow[:, cols].bitcast(FP8X4), scales=osc[:, cols], in_=ob[c][:].rearrange("p j t -> p (j t)"))
+
+        def store_w(c0, c1):
+            cols = slice(c0 * CH, c1 * CH)
+            nc.sync.dma_start(out_w[:, cols], ow[:, cols].bitcast(I32))
+
+        def clock(i, ap):
+            nc.gpsimd.tensor_copy(clk[:, 8 * i : 8 * i + 1], ap)
+
+        cast_w("w1", 1, "S")
+        cast_w("w1", 0, "V")
+        quant_w("w1", 0)
+        quant_w("w1", 1)
+        cast_w("w2", 1, "S")
+        cast_w("w2", 0, "V")
+        quant_w("w2", 0)
+        quant_w("w2", 1)
+        mm_y(0)
+        mm_y(1)
+        mm_y(2)
+        mm_y(3)
+        fifth(0)
+        fifth(1)
+        fifth(2)
+        fifth(3)
+        cast_w("w3", 0, "V")
+        cast_w("w3", 1, "V")
+        quant_w("w3", 0)
+        quant_w("w3", 1)
+        leaky(0)
+        leaky(1)
+        quant_h(0)
+        mm_e(0)
+        leaky(2)
+        quant_h(1)
+        mm_e(1)
+        leaky(3)
+        quant_h(2)
+        mm_e(2)
+        cast_w("w4", 0, "S")
+        cast_w("w4", 1, "S")
+        quant_w("w4", 0)
+        quant_h(3)
+        mm_e(3)
+        quant_w("w4", 1)
+        sig(0)
+        sig(1)
+        sig(2)
+        sig(3)
+        mm_v(0)
+        mm_v(1)
+        mm_v(2)
+        mm_v(3)
+        mul(0)
+        cast_o(0, "S")
+        mul(1)
+        cast_o(1, "S")
+        mul(2)
+        quant_o(0)
+        cast_o(2, "S")
+        mul(3)
+        quant_o(1)
+        store_w(0, 2)
+        cast_o(3, "V")
+        quant_o(2)
+        quant_o(3)
+        store_w(2, 4)
+        for q in range(4):
+            eng = nc.scalar if q % 2 == 0 else nc.sync
+            eng.dma_start(out_2[0, 4 * q : 4 * q + 4, :].bitcast(I32), osc[32 * q : 32 * q + 4, :].bitcast(I32))

@@ -146,9 +146,16 @@ def tile_picked_zgatt_sigmoid_po_kernel(tc, x_words, x_scales, w1, w2, w3, w4, o
             cols = slice(c0 * CH, c1 * CH)
             nc.sync.dma_start(out_w[:, cols], ow[:, cols].bitcast(I32))
 
+        def warm_pe(n):
+            spare = psum.tile([P, S], F32, name="spare", tag="b3")
+            for i in range(n):
+                nc.tensor.matmul_mx(out=spare[:], lhsT=gw["dst"][:, 0:P].bitcast(FP8X4), lhsT_scale=gs["dst"][:, 0:P],
+                                    rhs=gw["dst"][:].bitcast(FP8X4), rhs_scale=gs["dst"][:], start=True, stop=True)
+
         def clock(i, ap):
             nc.gpsimd.tensor_copy(clk[:, 8 * i : 8 * i + 1], ap)
 
+        warm_pe(3)
         cast_w("w1", 1, "S")
         cast_w("w1", 0, "V")
         quant_w("w1", 0)

@@ -80,9 +80,9 @@ def tile_picked_zgatt_sigmoid_po_kernel(tc, x_words, x_scales, w1, w2, w3, w4, o
             nc.vector.quantize_mx(out=codes[name, u][:].bitcast(FP8X4), scales=scales[name, u][:],
                                   in_=grouped[name, u][:].rearrange("p t m j -> p (t m j)"))
 
-        def mm(bank, t, name, rw, rs, start, stop):
+        def mm(acc, t, name, rw, rs, start, stop):
             cols = slice((t % 2) * P, (t % 2 + 1) * P)
-            nc.tensor.matmul_mx(out=bank[:, t, :], lhsT=codes[name, t // 2][:, cols].bitcast(FP8X4),
+            nc.tensor.matmul_mx(out=acc, lhsT=codes[name, t // 2][:, cols].bitcast(FP8X4),
                                 lhsT_scale=scales[name, t // 2][:, cols],
                                 rhs=rw.bitcast(FP8X4), rhs_scale=rs, start=start, stop=stop)
 
@@ -92,55 +92,68 @@ def tile_picked_zgatt_sigmoid_po_kernel(tc, x_words, x_scales, w1, w2, w3, w4, o
             cols = slice(c * CH, (c + 1) * CH)
             yb[c] = psum.tile([P, 4, CH], F32, name="ybank%d" % c, tag="a%d" % c)
             for t in range(4):
-                mm(yb[c], t, "w1", gw["offs"][:, cols], gs["offs"][:, cols], True, False)
-                mm(yb[c], t, "w2", gw["dst"][:, cols], gs["dst"][:, cols], False, True)
+                mm(yb[c][:, t, :], t, "w1", gw["offs"][:, cols], gs["offs"][:, cols], True, False)
+                mm(yb[c][:, t, :], t, "w2", gw["dst"][:, cols], gs["dst"][:, cols], False, True)
 
         def fifth(c):
             ya[c] = keep.tile([P, CH, 4], F32, name="a%d" % c)
             nc.scalar.activation(ya[c][:], yb[c][:].rearrange("p t j -> p j t"), ACT.Copy, scale=0.2)
 
+        HALF = S // 2
+        for h in range(2):
+            hb[h] = keep.tile([P, HALF, 4], BF16, name="hb%d" % h, align_bytes=64)
+            ob[h] = keep.tile([P, HALF, 4], BF16, name="ob%d" % h, align_bytes=64)
+            of[h] = keep.tile([P, 4, HALF], F32, name="o%d" % h, align_bytes=64)
+
         def leaky(c):
-            hb[c] = keep.tile([P, CH, 4], BF16, name="hb%d" % c, align_bytes=64)
-            nc.vector.tensor_tensor(hb[c][:], yb[c][:].rearrange("p t j -> p j t"), ya[c][:], ALU.max)
+            cols = slice((c % 2) * CH, (c % 2 + 1) * CH)
+            nc.vector.tensor_tensor(hb[c // 2][:, cols, :], yb[c][:].rearrange("p t j -> p j t"), ya[c][:], ALU.max)
 
-        def quant_h(c):
-            hq[c] = keep.tile([P, CH], U32, name="hq%d" % c, align_bytes=64)
-            hs[c] = keep.tile([P, CH], U8, name="hs%d" % c, align_bytes=64)
-            nc.vector.quantize_mx(out=hq[c][:].bitcast(FP8X4), scales=hs[c][:], in_=hb[c][:].rearrange("p j t -> p (j t)"))
+        def quant_h(h):
+            hq[h] = keep.tile([P, HALF], U32, name="hq%d" % h, align_bytes=64)
+            hs[h] = keep.tile([P, HALF], U8, name="hs%d" % h, align_bytes=64)
+            nc.vector.quantize_mx(out=hq[h][:].bitcast(FP8X4), scales=hs[h][:], in_=hb[h][:].rearrange("p j t -> p (j t)"))
 
-        def mm_e(c):
-            eb[c] = psum.tile([P, 4, CH], F32, name="ebank%d" % c, tag="b%d" % c)
-            for t in range(4):
-                mm(eb[c], t, "w3", hq[c][:], hs[c][:], True, True)
+        def mm_e(h, u):
+            eb[h, u] = psum.tile([P, 2, HALF], F32, name="ebank%d%d" % (h, u), tag="b%d" % (2 * h + u))
+            for i in range(2):
+                mm(eb[h, u][:, i, :], 2 * u + i, "w3", hq[h][:], hs[h][:], True, True)
 
-        def sig(c):
-            es[c] = keep.tile([P, 4, CH], F32, name="es%d" % c)
-            nc.scalar.activation(es[c][:], eb[c][:], ACT.Sigmoid)
+        def sig(h, u):
+            es[h, u] = keep.tile([P, 2, HALF], F32, name="es%d%d" % (h, u))
+            nc.scalar.activation(es[h, u][:], eb[h, u][:], ACT.Sigmoid)
 
         ow = keep.tile([P, S], U32, name="ow", align_bytes=64)
         osc = keep.tile([P, S], U8, name="osc", align_bytes=64)
         out_v = out_0.rearrange("(p t) j -> p t j", t=4)
         out_w = out_1[0].rearrange("p n t -> p (n t)").bitcast(I32)
 
-        def mm_v(c):
-            cols = slice(c * CH, (c + 1) * CH)
-            vb[c] = psum.tile([P, 4, CH], F32, name="vbank%d" % c, tag="a%d" % c)
-            for t in range(4):
-                mm(vb[c], t, "w4", gw["offs"][:, cols], gs["offs"][:, cols], True, True)
+        def mm_v(h, u):
+            cols = slice(h * HALF, (h + 1) * HALF)
+            vb[h, u] = psum.tile([P, 2, HALF], F32, name="vbank%d%d" % (h, u), tag="a%d" % (2 * h + u))
+            for i in range(2):
+                mm(vb[h, u][:, i, :], 2 * u + i, "w4", gw["offs"][:, cols], gs["offs"][:, cols], True, True)
 
-        def mul(c):
-            cols = slice(c * CH, (c + 1) * CH)
-            of[c] = keep.tile([P, 4, CH], F32, name="o%d" % c)
-            nc.vector.tensor_tensor(of[c][:], vb[c][:], es[c][:], ALU.mult)
-            nc.sync.dma_start(out_v[:, :, cols], of[c][:])
+        def mul(h, u):
+            cols = slice(h * HALF, (h + 1) * HALF)
+            pair = slice(2 * u, 2 * u + 2)
+            nc.vector.tensor_tensor(of[h][:, pair, :], vb[h, u][:], es[h, u][:], ALU.mult)
+            nc.sync.dma_start(out_v[:, pair, cols], of[h][:, pair, :])
 
         def cast_o(c, eng):
-            ob[c] = keep.tile([P, CH, 4], BF16, name="ob%d" % c, align_bytes=64)
-            copy_on(eng, ob[c][:].rearrange("p (c i) t -> p c t i", i=4), of[c][:].rearrange("p t (c i) -> p c t i", i=4))
+            cols = slice((c % 2) * CH, (c % 2 + 1) * CH)
+            if eng == "G":
+                copy_on(eng, ob[c // 2][:, cols, :], of[c // 2][:, :, cols].rearrange("p t j -> p j t"))
+            else:
+                copy_on(eng, ob[c // 2][:, cols, :].rearrange("p (c i) t -> p c t i", i=4),
+                        of[c // 2][:, :, cols].rearrange("p t (c i) -> p c t i", i=4))
 
-        def quant_o(c):
-            cols = slice(c * CH, (c + 1) * CH)
-            nc.vector.quantize_mx(out=ow[:, cols].bitcast(FP8X4), scales=osc[:, cols], in_=ob[c][:].rearrange("p j t -> p (j t)"))
+        def quant_o(c0, c1):
+            h = c0 // 2
+            cols = slice(c0 * CH, c1 * CH)
+            part = slice((c0 - 2 * h) * CH, (c1 - 2 * h) * CH)
+            nc.vector.quantize_mx(out=ow[:, cols].bitcast(FP8X4), scales=osc[:, cols],
+                                  in_=ob[h][:, part, :].rearrange("p j t -> p (j t)"))
 
         def store_w(c0, c1):
             cols = slice(c0 * CH, c1 * CH)
@@ -178,41 +191,37 @@ def tile_picked_zgatt_sigmoid_po_kernel(tc, x_words, x_scales, w1, w2, w3, w4, o
         quant_w("w3", 1)
         leaky(0)
         leaky(1)
-        quant_h(0)
-        mm_e(0)
         leaky(2)
-        quant_h(1)
-        mm_e(1)
+        quant_h(0)
+        mm_e(0, 0)
+        mm_e(0, 1)
         leaky(3)
-        quant_h(2)
-        mm_e(2)
         cast_w("w4", 0, "S")
         cast_w("w4", 1, "S")
         quant_w("w4", 0)
-        quant_h(3)
-        mm_e(3)
+        mm_v(0, 0)
+        quant_h(1)
+        mm_e(1, 0)
+        mm_e(1, 1)
         quant_w("w4", 1)
-        sig(0)
-        sig(1)
-        sig(2)
-        sig(3)
-        mm_v(0)
-        mm_v(1)
-        mm_v(2)
-        mm_v(3)
-        mul(0)
+        mm_v(0, 1)
+        mm_v(1, 0)
+        mm_v(1, 1)
+        sig(0, 0)
+        sig(0, 1)
+        sig(1, 0)
+        sig(1, 1)
+        mul(0, 0)
+        mul(0, 1)
         cast_o(0, "S")
-        mul(1)
         cast_o(1, "S")
-        mul(2)
-        quant_o(0)
+        mul(1, 0)
+        mul(1, 1)
         cast_o(2, "S")
-        mul(3)
-        quant_o(1)
-        store_w(0, 2)
         cast_o(3, "V")
-        quant_o(2)
-        quant_o(3)
+        quant_o(0, 2)
+        store_w(0, 2)
+        quant_o(2, 4)
         store_w(2, 4)
         for q in range(4):
             eng = nc.scalar if q % 2 == 0 else nc.sync

@@ -17,7 +17,7 @@ K = 512
 T = 2048
 S = 512
 CH = 128
-NCH = S // CH
+HALF = S // 2
 FLOPS = 4 * 2 * 512 * 512 * 512
 
 
@@ -27,38 +27,43 @@ def tile_picked_zgatt_sigmoid_po_kernel(tc, x_words, x_scales, w1, w2, w3, w4, o
         keep = ctx.enter_context(tc.tile_pool(name="keep", bufs=1))
         psum = ctx.enter_context(tc.psum_pool(name="psum", bufs=1))
 
-        offs_t = keep.tile([P, S // 16], U16, name="offs_t")
-        dst_t = keep.tile([P, S // 16], U16, name="dst_t")
+        lists = {"offs": keep.tile([P, S // 16], U16, name="offs_t"), "dst": keep.tile([P, S // 16], U16, name="dst_t")}
         xw = keep.tile([P, T], I32, name="xw", align_bytes=64)
         xs = keep.tile([P, T], U8, name="xs", align_bytes=64)
         warm = keep.tile([P, 8], F32, name="warm")
         warm2 = keep.tile([P, 8], F32, name="warm2")
-
-        nc.vector.memset(xs[:].bitcast(I32), 0)
-        nc.vector.memset(warm[:], 0.0)
-        nc.sync.dma_start(offs_t[:], offs)
-        nc.sync.dma_start(dst_t[:], dst)
         xw_hbm = x_words[0].rearrange("p n t -> p (n t)").bitcast(I32)
-        nc.sync.dma_start(xw[:, 0:512], xw_hbm[:, 0:512])
-        for q in range(4):
-            nc.sync.dma_start(xs[32 * q : 32 * q + 4, :].bitcast(I32), x_scales[0, 4 * q : 4 * q + 4, :].bitcast(I32))
-        nc.sync.dma_start(xw[:, 512:T], xw_hbm[:, 512:T])
-        nc.scalar.activation(warm2[:], warm[:], ACT.Sigmoid)
-        raw = {}
-        for name, w in (("w1", w1), ("w2", w2), ("w3", w3), ("w4", w4)):
-            raw[name] = keep.tile([P, 4, K], F32, name="raw_" + name, align_bytes=64)
-            nc.sync.dma_start(raw[name][:], w.rearrange("(p j) c -> p j c", j=4))
+        weights = {"w1": w1, "w2": w2, "w3": w3, "w4": w4}
+        raw, gw, gs, grouped, codes, scales = {}, {}, {}, {}, {}, {}
+        hq, hs, hb, yb, ya, eb, es, vb, of, ob = {}, {}, {}, {}, {}, {}, {}, {}, {}, {}
 
-        gw, gs = {}, {}
-        for name, lst in (("offs", offs_t), ("dst", dst_t)):
+        def load_lists():
+            nc.sync.dma_start(lists["offs"][:], offs)
+            nc.sync.dma_start(lists["dst"][:], dst)
+
+        def load_x(a, b):
+            nc.sync.dma_start(xw[:, a:b], xw_hbm[:, a:b])
+
+        def load_scales():
+            for q in range(4):
+                nc.sync.dma_start(xs[32 * q : 32 * q + 4, :].bitcast(I32), x_scales[0, 4 * q : 4 * q + 4, :].bitcast(I32))
+
+        def load_w(name, a=0, b=P):
+            raw[name, a] = keep.tile([P, 4, 4 * (b - a)], F32, name="raw_%s_%d" % (name, a), align_bytes=64)
+            nc.sync.dma_start(raw[name, a][:], weights[name].rearrange("(p j) c -> p j c", j=4)[:, :, 4 * a : 4 * b])
+
+        for name in ("offs", "dst"):
             gs[name] = keep.tile([P, S], U8, name="gs_" + name, align_bytes=64)
-            nc.vector.tensor_copy(gs[name][:], xs[:].indirect(lst[:]))
-        for name, lst in (("offs", offs_t), ("dst", dst_t)):
-            gw[name] = keep.tile([P, S], U32, name="gw_" + name, align_bytes=64)
-            nc.vector.tensor_copy(gw[name][:], xw[:].bitcast(U32).indirect(lst[:]))
 
-        grouped, codes, scales = {}, {}, {}
-        clk = keep.tile([P, 64], F32, name="clk")
+        def gather_s(name, a=0, b=S):
+            nc.vector.tensor_copy(gs[name][:, a:b], xs[:].indirect(lists[name][:, a // 16 : b // 16]))
+
+        def gather_w(name):
+            gw[name] = keep.tile([P, S], U32, name="gw_" + name, align_bytes=64)
+            nc.vector.tensor_copy(gw[name][:], xw[:].bitcast(U32).indirect(lists[name][:]))
+
+        def words(name, c):
+            return gw[name][:, c * CH : (c + 1) * CH]
 
         def copy_on(eng, out, in_):
             if eng == "V":
@@ -68,123 +73,157 @@ def tile_picked_zgatt_sigmoid_po_kernel(tc, x_words, x_scales, w1, w2, w3, w4, o
             else:
                 nc.gpsimd.tensor_scalar(out, in_, 1.0, 0.0, ALU.mult, ALU.add)
 
-        def cast_w(name, u, eng):
-            g = keep.tile([P, 2, P, 4], BF16, name="grp_%s_%d" % (name, u), align_bytes=64)
-            grouped[name, u] = g
-            src = raw[name][:].rearrange("p j (m t) -> p m j t", t=4)[:, :, :, 2 * u : 2 * u + 2]
-            copy_on(eng, g[:].rearrange("p t m j -> p m j t"), src)
+        def cast_w(name, u, eng, a=0, b=P, slots=2):
+            if (name, u) not in grouped:
+                grouped[name, u] = keep.tile([P, slots, P, 4], BF16, name="grp_%s_%d" % (name, u), align_bytes=64)
+            mine = slice(slots * u, slots * (u + 1))
+            if eng == "G":
+                src = raw[name, a][:].rearrange("p j (m t) -> p m t j", t=4)[:, :, mine, :]
+                copy_on(eng, grouped[name, u][:, :, a:b, :].rearrange("p t m j -> p m t j"), src)
+            else:
+                src = raw[name, a][:].rearrange("p j (m t) -> p m j t", t=4)[:, :, :, mine]
+                copy_on(eng, grouped[name, u][:, :, a:b, :].rearrange("p t m j -> p m j t"), src)
 
-        def quant_w(name, u):
-            codes[name, u] = keep.tile([P, 2 * P], U32, name="codes_%s_%d" % (name, u), align_bytes=64)
-            scales[name, u] = keep.tile([P, 2 * P], U8, name="scales_%s_%d" % (name, u), align_bytes=64)
-            nc.vector.quantize_mx(out=codes[name, u][:].bitcast(FP8X4), scales=scales[name, u][:],
+        def quant_w(name, u, slots=2):
+            if name not in codes:
+                codes[name] = keep.tile([P, K], U32, name="codes_" + name, align_bytes=64)
+                scales[name] = keep.tile([P, K], U8, name="scales_" + name, align_bytes=64)
+            cols = slice(slots * P * u, slots * P * (u + 1))
+            nc.vector.quantize_mx(out=codes[name][:, cols].bitcast(FP8X4), scales=scales[name][:, cols],
                                   in_=grouped[name, u][:].rearrange("p t m j -> p (t m j)"))
 
         def mm(acc, t, name, rw, rs, start, stop):
-            cols = slice((t % 2) * P, (t % 2 + 1) * P)
-            nc.tensor.matmul_mx(out=acc, lhsT=codes[name, t // 2][:, cols].bitcast(FP8X4),
-                                lhsT_scale=scales[name, t // 2][:, cols],
+            cols = slice(t * P, (t + 1) * P)
+            nc.tensor.matmul_mx(out=acc, lhsT=codes[name][:, cols].bitcast(FP8X4),
+                                lhsT_scale=scales[name][:, cols],
                                 rhs=rw.bitcast(FP8X4), rhs_scale=rs, start=start, stop=stop)
 
-        hq, hs, hb, yb, ya, eb, es, vb, of, ob = {}, {}, {}, {}, {}, {}, {}, {}, {}, {}
-
-        def mm_y(c):
+        def y_pass(c, t, second):
             cols = slice(c * CH, (c + 1) * CH)
-            yb[c] = psum.tile([P, 4, CH], F32, name="ybank%d" % c, tag="a%d" % c)
+            if c not in yb:
+                yb[c] = psum.tile([P, 4, CH], F32, name="ybank%d" % c, tag="a%d" % c)
+            if second:
+                mm(yb[c][:, t, :], t, "w2", words("dst", c), gs["dst"][:, cols], False, True)
+            else:
+                mm(yb[c][:, t, :], t, "w1", words("offs", c), gs["offs"][:, cols], True, False)
+
+        def open_y(c):
+            y_pass(c, 0, False)
+
+        def mm_y(c, opened):
             for t in range(4):
-                mm(yb[c][:, t, :], t, "w1", gw["offs"][:, cols], gs["offs"][:, cols], True, False)
-                mm(yb[c][:, t, :], t, "w2", gw["dst"][:, cols], gs["dst"][:, cols], False, True)
+                if t > 0 or not opened:
+                    y_pass(c, t, False)
+                y_pass(c, t, True)
 
         def fifth(c):
             ya[c] = keep.tile([P, CH, 4], F32, name="a%d" % c)
             nc.scalar.activation(ya[c][:], yb[c][:].rearrange("p t j -> p j t"), ACT.Copy, scale=0.2)
 
-        HALF = S // 2
         for h in range(2):
             hb[h] = keep.tile([P, HALF, 4], BF16, name="hb%d" % h, align_bytes=64)
             ob[h] = keep.tile([P, HALF, 4], BF16, name="ob%d" % h, align_bytes=64)
-            of[h] = keep.tile([P, 4, HALF], F32, name="o%d" % h, align_bytes=64)
-
-        def leaky(c):
-            cols = slice((c % 2) * CH, (c % 2 + 1) * CH)
-            nc.vector.tensor_tensor(hb[c // 2][:, cols, :], yb[c][:].rearrange("p t j -> p j t"), ya[c][:], ALU.max)
-
-        def quant_h(h):
-            hq[h] = keep.tile([P, HALF], U32, name="hq%d" % h, align_bytes=64)
-            hs[h] = keep.tile([P, HALF], U8, name="hs%d" % h, align_bytes=64)
-            nc.vector.quantize_mx(out=hq[h][:].bitcast(FP8X4), scales=hs[h][:], in_=hb[h][:].rearrange("p j t -> p (j t)"))
-
-        def mm_e(h, u):
-            eb[h, u] = psum.tile([P, 2, HALF], F32, name="ebank%d%d" % (h, u), tag="b%d" % (2 * h + u))
-            for i in range(2):
-                mm(eb[h, u][:, i, :], 2 * u + i, "w3", hq[h][:], hs[h][:], True, True)
-
-        def sig(h, u):
-            es[h, u] = keep.tile([P, 2, HALF], F32, name="es%d%d" % (h, u))
-            nc.scalar.activation(es[h, u][:], eb[h, u][:], ACT.Sigmoid)
-
+        hq = keep.tile([P, S], U32, name="hq", align_bytes=64)
+        hs = keep.tile([P, S], U8, name="hs", align_bytes=64)
         ow = keep.tile([P, S], U32, name="ow", align_bytes=64)
         osc = keep.tile([P, S], U8, name="osc", align_bytes=64)
         out_v = out_0.rearrange("(p t) j -> p t j", t=4)
         out_w = out_1[0].rearrange("p n t -> p (n t)").bitcast(I32)
 
-        def mm_v(h, u):
-            cols = slice(h * HALF, (h + 1) * HALF)
-            vb[h, u] = psum.tile([P, 2, HALF], F32, name="vbank%d%d" % (h, u), tag="a%d" % (2 * h + u))
-            for i in range(2):
-                mm(vb[h, u][:, i, :], 2 * u + i, "w4", gw["offs"][:, cols], gs["offs"][:, cols], True, True)
+        def part(c0, c1):
+            return slice((c0 % 2) * CH, (c0 % 2 + c1 - c0) * CH)
 
-        def mul(h, u):
-            cols = slice(h * HALF, (h + 1) * HALF)
-            pair = slice(2 * u, 2 * u + 2)
-            nc.vector.tensor_tensor(of[h][:, pair, :], vb[h, u][:], es[h, u][:], ALU.mult)
-            nc.sync.dma_start(out_v[:, pair, cols], of[h][:, pair, :])
+        def leaky(c):
+            nc.vector.tensor_tensor(hb[c // 2][:, part(c, c + 1), :], yb[c][:].rearrange("p t j -> p j t"), ya[c][:], ALU.max)
 
-        def cast_o(c, eng):
-            cols = slice((c % 2) * CH, (c % 2 + 1) * CH)
-            if eng == "G":
-                copy_on(eng, ob[c // 2][:, cols, :], of[c // 2][:, :, cols].rearrange("p t j -> p j t"))
-            else:
-                copy_on(eng, ob[c // 2][:, cols, :].rearrange("p (c i) t -> p c t i", i=4),
-                        of[c // 2][:, :, cols].rearrange("p t (c i) -> p c t i", i=4))
+        def quant_h(c0, c1):
+            cols = slice(c0 * CH, c1 * CH)
+            nc.vector.quantize_mx(out=hq[:, cols].bitcast(FP8X4), scales=hs[:, cols],
+                                  in_=hb[c0 // 2][:, part(c0, c1), :].rearrange("p j t -> p (j t)"))
+
+        pieces = [(0, 2, 0, HALF), (2, 4, 0, HALF), (0, 2, HALF, S), (2, 4, HALF, S)]
+        of[0] = keep.tile([P, 4, HALF], F32, name="o01", align_bytes=64)
+        of[1] = of[0]
+        of[2] = keep.tile([P, 4, HALF], F32, name="o23", align_bytes=64)
+        of[3] = of[2]
+
+        def mm_e(i):
+            t0, t1, a, b = pieces[i]
+            eb[i] = psum.tile([P, t1 - t0, b - a], F32, name="ebank%d" % i, tag="b%d" % i)
+            for t in range(t0, t1):
+                mm(eb[i][:, t - t0, :], t, "w3", hq[:, a:b], hs[:, a:b], True, True)
+
+        def sig(i):
+            t0, t1, a, b = pieces[i]
+            es[i] = keep.tile([P, t1 - t0, b - a], F32, name="es%d" % i)
+            nc.scalar.activation(es[i][:], eb[i][:], ACT.Sigmoid)
+
+        def mm_v(i):
+            t0, t1, a, b = pieces[i]
+            vb[i] = psum.tile([P, t1 - t0, b - a], F32, name="vbank%d" % i, tag="a%d" % i)
+            for t in range(t0, t1):
+                mm(vb[i][:, t - t0, :], t, "w4", gw["offs"][:, a:b], gs["offs"][:, a:b], True, True)
+
+        def mul(i):
+            t0, t1, a, b = pieces[i]
+            nc.vector.tensor_tensor(of[i][:, t0:t1, :], vb[i][:], es[i][:], ALU.mult)
+            nc.sync.dma_start(out_v[:, t0:t1, a:b], of[i][:, t0:t1, :])
+
+        def cast_o(h, a, b, eng):
+            copy_on(eng, ob[h][:, a:b, :].rearrange("p (c i) t -> p c t i", i=4),
+                    of[2 * h][:, :, a:b].rearrange("p t (c i) -> p c t i", i=4))
 
         def quant_o(c0, c1):
-            h = c0 // 2
             cols = slice(c0 * CH, c1 * CH)
-            part = slice((c0 - 2 * h) * CH, (c1 - 2 * h) * CH)
             nc.vector.quantize_mx(out=ow[:, cols].bitcast(FP8X4), scales=osc[:, cols],
-                                  in_=ob[h][:, part, :].rearrange("p j t -> p (j t)"))
+                                  in_=ob[c0 // 2][:, part(c0, c1), :].rearrange("p j t -> p (j t)"))
 
         def store_w(c0, c1):
             cols = slice(c0 * CH, c1 * CH)
             nc.sync.dma_start(out_w[:, cols], ow[:, cols].bitcast(I32))
 
-        def warm_pe(n):
-            spare = psum.tile([P, S], F32, name="spare", tag="b3")
-            for i in range(n):
-                nc.tensor.matmul_mx(out=spare[:], lhsT=gw["dst"][:, 0:P].bitcast(FP8X4), lhsT_scale=gs["dst"][:, 0:P],
-                                    rhs=gw["dst"][:].bitcast(FP8X4), rhs_scale=gs["dst"][:], start=True, stop=True)
+        def store_scales():
+            for q in range(4):
+                eng = nc.scalar if q % 2 == 0 else nc.sync
+                eng.dma_start(out_2[0, 4 * q : 4 * q + 4, :].bitcast(I32), osc[32 * q : 32 * q + 4, :].bitcast(I32))
 
-        def clock(i, ap):
-            nc.gpsimd.tensor_copy(clk[:, 8 * i : 8 * i + 1], ap)
+        def spare_pass(tag):
+            spare = psum.tile([P, S], F32, name="spare_" + tag, tag=tag)
+            nc.tensor.matmul_mx(out=spare[:], lhsT=gw["dst"][:, 0:P].bitcast(FP8X4), lhsT_scale=gs["dst"][:, 0:P],
+                                rhs=gw["dst"][:].bitcast(FP8X4), rhs_scale=gs["dst"][:], start=True, stop=True)
 
-        warm_pe(3)
-        cast_w("w1", 1, "S")
-        cast_w("w1", 0, "V")
+        nc.vector.memset(xs[:].bitcast(I32), 0)
+        nc.vector.memset(warm[:], 0.0)
+        nc.scalar.activation(warm2[:], warm[:], ACT.Sigmoid)
+        load_lists()
+        load_x(0, 512)
+        load_scales()
+        load_w("w1", 0, 64)
+        load_x(512, T)
+        load_w("w1", 64, P)
+        for name in ("w2", "w3", "w4"):
+            load_w(name)
+        gather_s("offs")
+        gather_s("dst")
+        gather_w("offs")
+        gather_w("dst")
+        for tag in ("b2", "b3"):
+            spare_pass(tag)
+        for a in (0, 64):
+            for u in range(2):
+                cast_w("w1", u, "S", a, a + 64)
         quant_w("w1", 0)
         quant_w("w1", 1)
+        for c in range(4):
+            open_y(c)
         cast_w("w2", 1, "S")
         cast_w("w2", 0, "V")
         quant_w("w2", 0)
         quant_w("w2", 1)
-        mm_y(0)
-        mm_y(1)
-        mm_y(2)
-        mm_y(3)
-        fifth(0)
-        fifth(1)
-        fifth(2)
-        fifth(3)
+        for c in range(4):
+            mm_y(c, True)
+        for c in range(4):
+            fifth(c)
         cast_w("w3", 0, "V")
         cast_w("w3", 1, "V")
         quant_w("w3", 0)
@@ -192,37 +231,33 @@ def tile_picked_zgatt_sigmoid_po_kernel(tc, x_words, x_scales, w1, w2, w3, w4, o
         leaky(0)
         leaky(1)
         leaky(2)
-        quant_h(0)
-        mm_e(0, 0)
-        mm_e(0, 1)
+        quant_h(0, 2)
+        mm_e(0)
+        mm_e(1)
         leaky(3)
         cast_w("w4", 0, "S")
         cast_w("w4", 1, "S")
         quant_w("w4", 0)
-        mm_v(0, 0)
-        quant_h(1)
-        mm_e(1, 0)
-        mm_e(1, 1)
+        mm_v(0)
+        quant_h(2, 4)
+        mm_e(2)
+        mm_e(3)
         quant_w("w4", 1)
-        mm_v(0, 1)
-        mm_v(1, 0)
-        mm_v(1, 1)
-        sig(0, 0)
-        sig(0, 1)
-        sig(1, 0)
-        sig(1, 1)
-        mul(0, 0)
-        mul(0, 1)
-        cast_o(0, "S")
-        cast_o(1, "S")
-        mul(1, 0)
-        mul(1, 1)
-        cast_o(2, "S")
-        cast_o(3, "V")
+        mm_v(1)
+        mm_v(2)
+        mm_v(3)
+        for c in range(4):
+            sig(c)
+        mul(0)
+        mul(1)
+        cast_o(0, 0, CH, "S")
+        cast_o(0, CH, HALF, "S")
+        mul(2)
+        mul(3)
         quant_o(0, 2)
         store_w(0, 2)
+        cast_o(1, 0, CH, "S")
+        cast_o(1, CH, HALF, "V")
         quant_o(2, 4)
         store_w(2, 4)
-        for q in range(4):
-            eng = nc.scalar if q % 2 == 0 else nc.sync
-            eng.dma_start(out_2[0, 4 * q : 4 * q + 4, :].bitcast(I32), osc[32 * q : 32 * q + 4, :].bitcast(I32))
+        store_scales()

@@ -226,14 +226,16 @@ def tile_picked_zgatt_sigmoid_po_kernel(tc, x_words, x_scales, w1, w2, w3, w4, o
             fifth(c)
         cast_w("w3", 0, "V")
         cast_w("w3", 1, "V")
-        quant_w("w3", 0)
-        quant_w("w3", 1)
         leaky(0)
+        spare_pass("a0")
+        quant_w("w3", 0)
         leaky(1)
-        leaky(2)
+        spare_pass("a1")
+        quant_w("w3", 1)
         quant_h(0, 2)
         mm_e(0)
         mm_e(1)
+        leaky(2)
         leaky(3)
         cast_w("w4", 0, "S")
         cast_w("w4", 1, "S")
@@ -241,10 +243,10 @@ def tile_picked_zgatt_sigmoid_po_kernel(tc, x_words, x_scales, w1, w2, w3, w4, o
         mm_v(0)
         quant_h(2, 4)
         mm_e(2)
-        mm_e(3)
         quant_w("w4", 1)
         mm_v(1)
         mm_v(2)
+        mm_e(3)
         mm_v(3)
         for c in range(4):
             sig(c)

@@ -198,10 +198,8 @@ def tile_picked_zgatt_sigmoid_po_kernel(tc, x_words, x_scales, w1, w2, w3, w4, o
         load_lists()
         load_x(0, 512)
         load_scales()
-        load_w("w1", 0, 64)
         load_x(512, T)
-        load_w("w1", 64, P)
-        for name in ("w2", "w3", "w4"):
+        for name in ("w1", "w2", "w3", "w4"):
             load_w(name)
         gather_s("offs")
         gather_s("dst")
@@ -209,9 +207,8 @@ def tile_picked_zgatt_sigmoid_po_kernel(tc, x_words, x_scales, w1, w2, w3, w4, o
         gather_w("dst")
         for tag in ("b2", "b3"):
             spare_pass(tag)
-        for a in (0, 64):
-            for u in range(2):
-                cast_w("w1", u, "S", a, a + 64)
+        cast_w("w1", 1, "S")
+        cast_w("w1", 0, "V")
         quant_w("w1", 0)
         quant_w("w1", 1)
         for c in range(4):

@@ -48,9 +48,10 @@ def tile_picked_zgatt_sigmoid_po_kernel(tc, x_words, x_scales, w1, w2, w3, w4, o
             for q in range(4):
                 nc.sync.dma_start(xs[32 * q : 32 * q + 4, :].bitcast(I32), x_scales[0, 4 * q : 4 * q + 4, :].bitcast(I32))
 
-        def load_w(name, a=0, b=P):
-            raw[name, a] = keep.tile([P, 4, 4 * (b - a)], F32, name="raw_%s_%d" % (name, a), align_bytes=64)
-            nc.sync.dma_start(raw[name, a][:], weights[name].rearrange("(p j) c -> p j c", j=4)[:, :, 4 * a : 4 * b])
+        def load_w(name, j0=0, j1=4):
+            if (name, 0) not in raw:
+                raw[name, 0] = keep.tile([P, 4, K], F32, name="raw_%s" % name, align_bytes=64)
+            nc.sync.dma_start(raw[name, 0][:, j0:j1, :], weights[name].rearrange("(p j) c -> p j c", j=4)[:, j0:j1, :])
 
         for name in ("offs", "dst"):
             gs[name] = keep.tile([P, S], U8, name="gs_" + name, align_bytes=64)
@@ -58,12 +59,12 @@ def tile_picked_zgatt_sigmoid_po_kernel(tc, x_words, x_scales, w1, w2, w3, w4, o
         def gather_s(name, a=0, b=S):
             nc.vector.tensor_copy(gs[name][:, a:b], xs[:].indirect(lists[name][:, a // 16 : b // 16]))
 
-        def gather_w(name):
-            gw[name] = keep.tile([P, S], U32, name="gw_" + name, align_bytes=64)
-            nc.vector.tensor_copy(gw[name][:], xw[:].bitcast(U32).indirect(lists[name][:]))
+        def gather_w(name, h, tag=None):
+            gw[name, h] = keep.tile([P, HALF], U32, name="gw_%s%d" % (name, h), tag=tag or "gw_%s%d" % (name, h), align_bytes=64)
+            nc.vector.tensor_copy(gw[name, h][:], xw[:].bitcast(U32).indirect(lists[name][:, h * HALF // 16 : (h + 1) * HALF // 16]))
 
         def words(name, c):
-            return gw[name][:, c * CH : (c + 1) * CH]
+            return gw[name, c // 2][:, (c % 2) * CH : (c % 2 + 1) * CH]
 
         def copy_on(eng, out, in_):
             if eng == "V":
@@ -75,7 +76,7 @@ def tile_picked_zgatt_sigmoid_po_kernel(tc, x_words, x_scales, w1, w2, w3, w4, o
 
         def cast_w(name, u, eng, a=0, b=P, slots=2):
             if (name, u) not in grouped:
-                grouped[name, u] = keep.tile([P, slots, P, 4], BF16, name="grp_%s_%d" % (name, u), align_bytes=64)
+                grouped[name, u] = keep.tile([P, slots, P, 4], BF16, name="grp_%s_%d" % (name, u), tag="grp_%s_%d" % (name, u), align_bytes=64)
             mine = slice(slots * u, slots * (u + 1))
             if eng == "G":
                 src = raw[name, a][:].rearrange("p j (m t) -> p m t j", t=4)[:, :, mine, :]
@@ -98,30 +99,21 @@ def tile_picked_zgatt_sigmoid_po_kernel(tc, x_words, x_scales, w1, w2, w3, w4, o
                                 lhsT_scale=scales[name][:, cols],
                                 rhs=rw.bitcast(FP8X4), rhs_scale=rs, start=start, stop=stop)
 
-        def y_pass(c, t, second):
+        done = {c: 0 for c in range(4)}
+
+        def y_pass(c, name, t):
             cols = slice(c * CH, (c + 1) * CH)
             if c not in yb:
                 yb[c] = psum.tile([P, 4, CH], F32, name="ybank%d" % c, tag="a%d" % c)
-            if second:
-                mm(yb[c][:, t, :], t, "w2", words("dst", c), gs["dst"][:, cols], False, True)
-            else:
-                mm(yb[c][:, t, :], t, "w1", words("offs", c), gs["offs"][:, cols], True, False)
-
-        def open_y(c):
-            y_pass(c, 0, False)
-
-        def mm_y(c, opened):
-            for t in range(4):
-                if t > 0 or not opened:
-                    y_pass(c, t, False)
-                y_pass(c, t, True)
+            lst = "offs" if name == "w1" else "dst"
+            mm(yb[c][:, t, :], t, name, words(lst, c), gs[lst][:, cols], done[c] == 0, done[c] == 7)
+            done[c] = done[c] + 1
 
         def fifth(c):
             ya[c] = keep.tile([P, CH, 4], F32, name="a%d" % c)
             nc.scalar.activation(ya[c][:], yb[c][:].rearrange("p t j -> p j t"), ACT.Copy, scale=0.2)
 
         for h in range(2):
-            hb[h] = keep.tile([P, HALF, 4], BF16, name="hb%d" % h, align_bytes=64)
             ob[h] = keep.tile([P, HALF, 4], BF16, name="ob%d" % h, align_bytes=64)
         hq = keep.tile([P, S], U32, name="hq", align_bytes=64)
         hs = keep.tile([P, S], U8, name="hs", align_bytes=64)
@@ -134,6 +126,8 @@ def tile_picked_zgatt_sigmoid_po_kernel(tc, x_words, x_scales, w1, w2, w3, w4, o
             return slice((c0 % 2) * CH, (c0 % 2 + c1 - c0) * CH)
 
         def leaky(c):
+            if c % 2 == 0:
+                hb[c // 2] = keep.tile([P, HALF, 4], BF16, name="hb%d" % (c // 2), tag="hb%d" % (c // 2), align_bytes=64)
             nc.vector.tensor_tensor(hb[c // 2][:, part(c, c + 1), :], yb[c][:].rearrange("p t j -> p j t"), ya[c][:], ALU.max)
 
         def quant_h(c0, c1):
@@ -162,7 +156,7 @@ def tile_picked_zgatt_sigmoid_po_kernel(tc, x_words, x_scales, w1, w2, w3, w4, o
             t0, t1, a, b = pieces[i]
             vb[i] = psum.tile([P, t1 - t0, b - a], F32, name="vbank%d" % i, tag="a%d" % i)
             for t in range(t0, t1):
-                mm(vb[i][:, t - t0, :], t, "w4", gw["offs"][:, a:b], gs["offs"][:, a:b], True, True)
+                mm(vb[i][:, t - t0, :], t, "w4", gw["offs", a // HALF][:], gs["offs"][:, a:b], True, True)
 
         def mul(i):
             t0, t1, a, b = pieces[i]
@@ -187,47 +181,51 @@ def tile_picked_zgatt_sigmoid_po_kernel(tc, x_words, x_scales, w1, w2, w3, w4, o
                 eng = nc.scalar if q % 2 == 0 else nc.sync
                 eng.dma_start(out_2[0, 4 * q : 4 * q + 4, :].bitcast(I32), osc[32 * q : 32 * q + 4, :].bitcast(I32))
 
-        def spare_pass(tag):
-            spare = psum.tile([P, S], F32, name="spare_" + tag, tag=tag)
-            nc.tensor.matmul_mx(out=spare[:], lhsT=gw["dst"][:, 0:P].bitcast(FP8X4), lhsT_scale=gs["dst"][:, 0:P],
-                                rhs=gw["dst"][:].bitcast(FP8X4), rhs_scale=gs["dst"][:], start=True, stop=True)
+        def spare_pass(tag, n):
+            spare = psum.tile([P, n], F32, name="spare_" + tag, tag=tag)
+            mm(spare[:], 0, "w1", codes["w2"][:, 0:n], scales["w2"][:, 0:n], True, True)
 
         nc.vector.memset(xs[:].bitcast(I32), 0)
         nc.vector.memset(warm[:], 0.0)
         nc.scalar.activation(warm2[:], warm[:], ACT.Sigmoid)
         load_lists()
-        load_x(0, 512)
+        load_w("w1", 0, 1)
         load_scales()
-        load_x(512, T)
-        for name in ("w1", "w2", "w3", "w4"):
+        load_w("w1", 1, 4)
+        load_x(0, T)
+        for name in ("w2", "w3", "w4"):
             load_w(name)
         gather_s("offs")
         gather_s("dst")
-        gather_w("offs")
-        gather_w("dst")
-        for tag in ("b2", "b3"):
-            spare_pass(tag)
         cast_w("w1", 1, "S")
         cast_w("w1", 0, "V")
         quant_w("w1", 0)
         quant_w("w1", 1)
-        for c in range(4):
-            open_y(c)
+        gather_w("offs", 0)
+        gather_w("offs", 1)
+        gather_w("dst", 0)
+        for c in range(3):
+            for t in range(4):
+                y_pass(c, "w1", t)
         cast_w("w2", 1, "S")
         cast_w("w2", 0, "V")
         quant_w("w2", 0)
         quant_w("w2", 1)
+        gather_w("dst", 1, "grp_w2_1")
         for c in range(4):
-            mm_y(c, True)
+            for t in (0, 1, 2, 3) if c == 0 else (3, 2, 1, 0):
+                y_pass(c, "w2", t)
+        for t in range(4):
+            y_pass(3, "w1", t)
         for c in range(4):
             fifth(c)
         cast_w("w3", 0, "V")
         cast_w("w3", 1, "V")
         leaky(0)
-        spare_pass("a0")
+        spare_pass("a0", 512)
         quant_w("w3", 0)
         leaky(1)
-        spare_pass("a1")
+        spare_pass("a1", 256)
         quant_w("w3", 1)
         quant_h(0, 2)
         mm_e(0)

@@ -79,10 +79,10 @@ def tile_picked_zgatt_sigmoid_po_kernel(tc, x_words, x_scales, w1, w2, w3, w4, o
                 grouped[name, u] = keep.tile([P, slots, P, 4], BF16, name="grp_%s_%d" % (name, u), tag="grp_%s_%d" % (name, u), align_bytes=64)
             mine = slice(slots * u, slots * (u + 1))
             if eng == "G":
-                src = raw[name, a][:].rearrange("p j (m t) -> p m t j", t=4)[:, :, mine, :]
+                src = raw[name, 0][:].rearrange("p j (m t) -> p m t j", t=4)[:, a:b, mine, :]
                 copy_on(eng, grouped[name, u][:, :, a:b, :].rearrange("p t m j -> p m t j"), src)
             else:
-                src = raw[name, a][:].rearrange("p j (m t) -> p m j t", t=4)[:, :, :, mine]
+                src = raw[name, 0][:].rearrange("p j (m t) -> p m j t", t=4)[:, a:b, :, mine]
                 copy_on(eng, grouped[name, u][:, :, a:b, :].rearrange("p t m j -> p m j t"), src)
 
         def quant_w(name, u, slots=2):
@@ -158,10 +158,11 @@ def tile_picked_zgatt_sigmoid_po_kernel(tc, x_words, x_scales, w1, w2, w3, w4, o
             for t in range(t0, t1):
                 mm(vb[i][:, t - t0, :], t, "w4", gw["offs", a // HALF][:], gs["offs"][:, a:b], True, True)
 
-        def mul(i):
+        def mul(i, lo=0, hi=HALF):
             t0, t1, a, b = pieces[i]
-            nc.vector.tensor_tensor(of[i][:, t0:t1, :], vb[i][:], es[i][:], ALU.mult)
-            nc.sync.dma_start(out_v[:, t0:t1, a:b], of[i][:, t0:t1, :])
+            nc.vector.tensor_tensor(of[i][:, t0:t1, lo:hi], vb[i][:, :, lo:hi], es[i][:, :, lo:hi], ALU.mult)
+            if hi == HALF:
+                nc.sync.dma_start(out_v[:, t0:t1, a:b], of[i][:, t0:t1, :])
 
         def cast_o(h, a, b, eng):
             copy_on(eng, ob[h][:, a:b, :].rearrange("p (c i) t -> p c t i", i=4),
@@ -197,16 +198,16 @@ def tile_picked_zgatt_sigmoid_po_kernel(tc, x_words, x_scales, w1, w2, w3, w4, o
             load_w(name)
         gather_s("offs")
         gather_s("dst")
-        cast_w("w1", 1, "S")
-        cast_w("w1", 0, "V")
+        cast_w("w1", 0, "S")
+        cast_w("w1", 1, "S", 48, P)
+        cast_w("w1", 1, "V", 0, 48)
         quant_w("w1", 0)
-        quant_w("w1", 1)
         gather_w("offs", 0)
+        quant_w("w1", 1)
         gather_w("offs", 1)
         gather_w("dst", 0)
-        for c in range(3):
-            for t in range(4):
-                y_pass(c, "w1", t)
+        for c, t in [(c, t) for t in range(4) for c in (0, 1)] + [(2, t) for t in range(4)]:
+            y_pass(c, "w1", t)
         cast_w("w2", 1, "S")
         cast_w("w2", 0, "V")
         quant_w("w2", 0)
@@ -247,14 +248,16 @@ def tile_picked_zgatt_sigmoid_po_kernel(tc, x_words, x_scales, w1, w2, w3, w4, o
             sig(c)
         mul(0)
         mul(1)
-        cast_o(0, 0, CH, "S")
-        cast_o(0, CH, HALF, "S")
+        cast_o(0, 0, HALF, "S")
         mul(2)
-        mul(3)
+        mul(3, 0, CH)
+        mul(3, CH, HALF)
+        cast_o(1, 0, CH, "V")
+        cast_o(1, CH, CH + 64, "V")
+        cast_o(1, CH + 64, HALF, "S")
+        quant_o(2, 3)
         quant_o(0, 2)
         store_w(0, 2)
-        cast_o(1, 0, CH, "S")
-        cast_o(1, CH, HALF, "V")
-        quant_o(2, 4)
+        quant_o(3, 4)
         store_w(2, 4)
         store_scales()

@@ -206,13 +206,13 @@ def tile_picked_zgatt_sigmoid_po_kernel(tc, x_words, x_scales, w1, w2, w3, w4, o
         quant_w("w1", 1)
         gather_w("offs", 1)
         gather_w("dst", 0)
+        gather_w("dst", 1)
         for c, t in [(c, t) for t in range(4) for c in (0, 1)] + [(2, t) for t in range(4)]:
             y_pass(c, "w1", t)
         cast_w("w2", 1, "S")
         cast_w("w2", 0, "V")
         quant_w("w2", 0)
         quant_w("w2", 1)
-        gather_w("dst", 1, "grp_w2_1")
         for c in range(4):
             for t in (0, 1, 2, 3) if c == 0 else (3, 2, 1, 0):
                 y_pass(c, "w2", t)

@@ -59,12 +59,16 @@ def tile_picked_zgatt_sigmoid_po_kernel(tc, x_words, x_scales, w1, w2, w3, w4, o
         def gather_s(name, a=0, b=S):
             nc.vector.tensor_copy(gs[name][:, a:b], xs[:].indirect(lists[name][:, a // 16 : b // 16]))
 
-        def gather_w(name, h, tag=None):
-            gw[name, h] = keep.tile([P, HALF], U32, name="gw_%s%d" % (name, h), tag=tag or "gw_%s%d" % (name, h), align_bytes=64)
-            nc.vector.tensor_copy(gw[name, h][:], xw[:].bitcast(U32).indirect(lists[name][:, h * HALF // 16 : (h + 1) * HALF // 16]))
+        def gather_w(name, c0, c1, tag=None):
+            mine = "gw_%s%d" % (name, c0)
+            tile = keep.tile([P, (c1 - c0) * CH], U32, name=mine, tag=tag or mine, align_bytes=64)
+            nc.vector.tensor_copy(tile[:], xw[:].bitcast(U32).indirect(lists[name][:, c0 * CH // 16 : c1 * CH // 16]))
+            for c in range(c0, c1):
+                gw[name, c] = (tile, c0)
 
-        def words(name, c):
-            return gw[name, c // 2][:, (c % 2) * CH : (c % 2 + 1) * CH]
+        def words(name, c, n=1):
+            tile, c0 = gw[name, c]
+            return tile[:, (c - c0) * CH : (c - c0 + n) * CH]
 
         def copy_on(eng, out, in_):
             if eng == "V":
@@ -76,7 +80,7 @@ def tile_picked_zgatt_sigmoid_po_kernel(tc, x_words, x_scales, w1, w2, w3, w4, o
 
         def cast_w(name, u, eng, a=0, b=P, slots=2):
             if (name, u) not in grouped:
-                grouped[name, u] = keep.tile([P, slots, P, 4], BF16, name="grp_%s_%d" % (name, u), tag="grp_%s_%d" % (name, u), align_bytes=64)
+                grouped[name, u] = keep.tile([P, slots, P, 4], BF16, name="grp_%s_%d" % (name, u), tag="ya0" if (name, u) == ("w3", 1) else "grp_%s_%d" % (name, u), align_bytes=64)
             mine = slice(slots * u, slots * (u + 1))
             if eng == "G":
                 src = raw[name, 0][:].rearrange("p j (m t) -> p m t j", t=4)[:, a:b, mine, :]
@@ -104,13 +108,13 @@ def tile_picked_zgatt_sigmoid_po_kernel(tc, x_words, x_scales, w1, w2, w3, w4, o
         def y_pass(c, name, t):
             cols = slice(c * CH, (c + 1) * CH)
             if c not in yb:
-                yb[c] = psum.tile([P, 4, CH], F32, name="ybank%d" % c, tag="a%d" % c)
+                yb[c] = psum.tile([P, 4, CH], F32, name="ybank%d" % c, tag="a%d" % (c % 3))
             lst = "offs" if name == "w1" else "dst"
             mm(yb[c][:, t, :], t, name, words(lst, c), gs[lst][:, cols], done[c] == 0, done[c] == 7)
             done[c] = done[c] + 1
 
         def fifth(c):
-            ya[c] = keep.tile([P, CH, 4], F32, name="a%d" % c)
+            ya[c] = keep.tile([P, CH, 4], F32, name="ya%d" % c, tag="ya%d" % c, align_bytes=64)
             nc.scalar.activation(ya[c][:], yb[c][:].rearrange("p t j -> p j t"), ACT.Copy, scale=0.2)
 
         for h in range(2):
@@ -154,9 +158,9 @@ def tile_picked_zgatt_sigmoid_po_kernel(tc, x_words, x_scales, w1, w2, w3, w4, o
 
         def mm_v(i):
             t0, t1, a, b = pieces[i]
-            vb[i] = psum.tile([P, t1 - t0, b - a], F32, name="vbank%d" % i, tag="a%d" % i)
+            vb[i] = psum.tile([P, t1 - t0, b - a], F32, name="vbank%d" % i, tag=("a3", "a1", "a2", "a0")[i])
             for t in range(t0, t1):
-                mm(vb[i][:, t - t0, :], t, "w4", gw["offs", a // HALF][:], gs["offs"][:, a:b], True, True)
+                mm(vb[i][:, t - t0, :], t, "w4", words("offs", a // CH, 2), gs["offs"][:, a:b], True, True)
 
         def mul(i, lo=0, hi=HALF):
             t0, t1, a, b = pieces[i]
@@ -182,10 +186,6 @@ def tile_picked_zgatt_sigmoid_po_kernel(tc, x_words, x_scales, w1, w2, w3, w4, o
                 eng = nc.scalar if q % 2 == 0 else nc.sync
                 eng.dma_start(out_2[0, 4 * q : 4 * q + 4, :].bitcast(I32), osc[32 * q : 32 * q + 4, :].bitcast(I32))
 
-        def spare_pass(tag, n):
-            spare = psum.tile([P, n], F32, name="spare_" + tag, tag=tag)
-            mm(spare[:], 0, "w1", codes["w2"][:, 0:n], scales["w2"][:, 0:n], True, True)
-
         nc.vector.memset(xs[:].bitcast(I32), 0)
         nc.vector.memset(warm[:], 0.0)
         nc.scalar.activation(warm2[:], warm[:], ACT.Sigmoid)
@@ -198,51 +198,53 @@ def tile_picked_zgatt_sigmoid_po_kernel(tc, x_words, x_scales, w1, w2, w3, w4, o
             load_w(name)
         gather_s("offs")
         gather_s("dst")
-        cast_w("w1", 0, "S")
-        cast_w("w1", 1, "S", 48, P)
-        cast_w("w1", 1, "V", 0, 48)
+        cast_w("w1", 1, "S")
+        cast_w("w1", 0, "V")
         quant_w("w1", 0)
-        gather_w("offs", 0)
         quant_w("w1", 1)
-        gather_w("offs", 1)
-        gather_w("dst", 0)
-        gather_w("dst", 1)
+        gather_w("offs", 0, 2)
+        gather_w("offs", 2, 4)
+        gather_w("dst", 0, 3)
         for c, t in [(c, t) for t in range(4) for c in (0, 1)] + [(2, t) for t in range(4)]:
             y_pass(c, "w1", t)
-        cast_w("w2", 1, "S")
-        cast_w("w2", 0, "V")
+        cast_w("w2", 0, "S", 64, P)
+        cast_w("w2", 1, "S", 80, P)
+        cast_w("w2", 0, "V", 0, 64)
+        cast_w("w2", 1, "V", 0, 80)
         quant_w("w2", 0)
         quant_w("w2", 1)
-        for c in range(4):
+        gather_w("dst", 3, 4, "grp_w2_1")
+        for c in range(3):
             for t in (0, 1, 2, 3) if c == 0 else (3, 2, 1, 0):
                 y_pass(c, "w2", t)
-        for t in range(4):
-            y_pass(3, "w1", t)
-        for c in range(4):
-            fifth(c)
+        fifth(0)
+        fifth(1)
+        fifth(2)
         cast_w("w3", 0, "V")
-        cast_w("w3", 1, "V")
         leaky(0)
-        spare_pass("a0", 512)
+        for name in ("w1", "w2"):
+            for t in range(4):
+                y_pass(3, name, t)
+        cast_w("w3", 1, "S")
         quant_w("w3", 0)
         leaky(1)
-        spare_pass("a1", 256)
-        quant_w("w3", 1)
+        leaky(2)
         quant_h(0, 2)
         mm_e(0)
+        quant_w("w3", 1)
         mm_e(1)
-        leaky(2)
-        leaky(3)
-        cast_w("w4", 0, "S")
+        cast_w("w4", 0, "V")
+        fifth(3)
         cast_w("w4", 1, "S")
+        leaky(3)
         quant_w("w4", 0)
         mm_v(0)
         quant_h(2, 4)
         mm_e(2)
         quant_w("w4", 1)
         mm_v(1)
-        mm_v(2)
         mm_e(3)
+        mm_v(2)
         mm_v(3)
         for c in range(4):
             sig(c)

@@ -225,7 +225,8 @@ def tile_picked_zgatt_sigmoid_po_kernel(tc, x_words, x_scales, w1, w2, w3, w4, o
         for name in ("w1", "w2"):
             for t in range(4):
                 y_pass(3, name, t)
-        cast_w("w3", 1, "S")
+        cast_w("w3", 1, "G", 64, P)
+        cast_w("w3", 1, "S", 0, 64)
         quant_w("w3", 0)
         leaky(1)
         leaky(2)
@@ -233,8 +234,9 @@ def tile_picked_zgatt_sigmoid_po_kernel(tc, x_words, x_scales, w1, w2, w3, w4, o
         mm_e(0)
         quant_w("w3", 1)
         mm_e(1)
-        cast_w("w4", 0, "V")
+        cast_w("w4", 0, "V", 0, 80)
         fifth(3)
+        cast_w("w4", 0, "S", 80, P)
         cast_w("w4", 1, "S")
         leaky(3)
         quant_w("w4", 0)

@@ -48,10 +48,10 @@ def tile_picked_zgatt_sigmoid_po_kernel(tc, x_words, x_scales, w1, w2, w3, w4, o
             for q in range(4):
                 nc.sync.dma_start(xs[32 * q : 32 * q + 4, :].bitcast(I32), x_scales[0, 4 * q : 4 * q + 4, :].bitcast(I32))
 
-        def load_w(name, j0=0, j1=4):
+        def load_w(name, j0=0, j1=4, c0=0, c1=K):
             if (name, 0) not in raw:
                 raw[name, 0] = keep.tile([P, 4, K], F32, name="raw_%s" % name, align_bytes=64)
-            nc.sync.dma_start(raw[name, 0][:, j0:j1, :], weights[name].rearrange("(p j) c -> p j c", j=4)[:, j0:j1, :])
+            nc.sync.dma_start(raw[name, 0][:, j0:j1, c0:c1], weights[name].rearrange("(p j) c -> p j c", j=4)[:, j0:j1, c0:c1])
 
         for name in ("offs", "dst"):
             gs[name] = keep.tile([P, S], U8, name="gs_" + name, align_bytes=64)
@@ -78,9 +78,11 @@ def tile_picked_zgatt_sigmoid_po_kernel(tc, x_words, x_scales, w1, w2, w3, w4, o
             else:
                 nc.gpsimd.tensor_scalar(out, in_, 1.0, 0.0, ALU.mult, ALU.add)
 
+        held_behind = {("w3", 1): "grp_w3_0", ("w4", 1): "hb0"}
+
         def cast_w(name, u, eng, a=0, b=P, slots=2):
             if (name, u) not in grouped:
-                grouped[name, u] = keep.tile([P, slots, P, 4], BF16, name="grp_%s_%d" % (name, u), tag="ya0" if (name, u) == ("w3", 1) else "grp_%s_%d" % (name, u), align_bytes=64)
+                grouped[name, u] = keep.tile([P, slots, P, 4], BF16, name="grp_%s_%d" % (name, u), tag=held_behind.get((name, u), "grp_%s_%d" % (name, u)), align_bytes=64)
             mine = slice(slots * u, slots * (u + 1))
             if eng == "G":
                 src = raw[name, 0][:].rearrange("p j (m t) -> p m t j", t=4)[:, a:b, mine, :]
@@ -169,6 +171,9 @@ def tile_picked_zgatt_sigmoid_po_kernel(tc, x_words, x_scales, w1, w2, w3, w4, o
                 nc.sync.dma_start(out_v[:, t0:t1, a:b], of[i][:, t0:t1, :])
 
         def cast_o(h, a, b, eng):
+            if eng == "G":
+                copy_on(eng, ob[h][:, a:b, :], of[2 * h][:, :, a:b].rearrange("p t j -> p j t"))
+                return
             copy_on(eng, ob[h][:, a:b, :].rearrange("p (c i) t -> p c t i", i=4),
                     of[2 * h][:, :, a:b].rearrange("p t (c i) -> p c t i", i=4))
 
@@ -195,7 +200,8 @@ def tile_picked_zgatt_sigmoid_po_kernel(tc, x_words, x_scales, w1, w2, w3, w4, o
         load_w("w1", 1, 4)
         load_x(0, T)
         for name in ("w2", "w3", "w4"):
-            load_w(name)
+            load_w(name, c1=K // 2)
+            load_w(name, c0=K // 2)
         gather_s("offs")
         gather_s("dst")
         cast_w("w1", 1, "S")
@@ -204,41 +210,44 @@ def tile_picked_zgatt_sigmoid_po_kernel(tc, x_words, x_scales, w1, w2, w3, w4, o
         quant_w("w1", 1)
         gather_w("offs", 0, 2)
         gather_w("offs", 2, 4)
-        gather_w("dst", 0, 3)
+        gather_w("dst", 0, 2)
         for c, t in [(c, t) for t in range(4) for c in (0, 1)] + [(2, t) for t in range(4)]:
             y_pass(c, "w1", t)
-        cast_w("w2", 0, "S", 64, P)
+        cast_w("w2", 0, "S", 0, 64)
+        cast_w("w2", 1, "S", 0, 64)
+        cast_w("w2", 0, "V", 64, P)
+        cast_w("w2", 1, "V", 64, 80)
         cast_w("w2", 1, "S", 80, P)
-        cast_w("w2", 0, "V", 0, 64)
-        cast_w("w2", 1, "V", 0, 80)
         quant_w("w2", 0)
         quant_w("w2", 1)
-        gather_w("dst", 3, 4, "grp_w2_1")
+        gather_w("dst", 2, 4, "grp_w2_1")
         for c in range(3):
             for t in (0, 1, 2, 3) if c == 0 else (3, 2, 1, 0):
                 y_pass(c, "w2", t)
+        cast_w("w3", 0, "S", 0, 64)
         fifth(0)
         fifth(1)
         fifth(2)
-        cast_w("w3", 0, "V")
+        cast_w("w3", 0, "V", 64, P)
+        quant_w("w3", 0)
+        cast_w("w3", 1, "G")
         leaky(0)
         for name in ("w1", "w2"):
             for t in range(4):
                 y_pass(3, name, t)
-        cast_w("w3", 1, "G", 64, P)
-        cast_w("w3", 1, "S", 0, 64)
-        quant_w("w3", 0)
         leaky(1)
         leaky(2)
+        cast_w("w4", 0, "S", 0, 64)
         quant_h(0, 2)
         mm_e(0)
         quant_w("w3", 1)
         mm_e(1)
-        cast_w("w4", 0, "V", 0, 80)
         fifth(3)
-        cast_w("w4", 0, "S", 80, P)
-        cast_w("w4", 1, "S")
+        cast_w("w4", 1, "G", 0, 40)
+        cast_w("w4", 0, "S", 64, P)
         leaky(3)
+        cast_w("w4", 1, "S", 40, 88)
+        cast_w("w4", 1, "V", 88, P)
         quant_w("w4", 0)
         mm_v(0)
         quant_h(2, 4)

@@ -78,7 +78,7 @@ def tile_picked_zgatt_sigmoid_po_kernel(tc, x_words, x_scales, w1, w2, w3, w4, o
             else:
                 nc.gpsimd.tensor_scalar(out, in_, 1.0, 0.0, ALU.mult, ALU.add)
 
-        held_behind = {("w3", 1): "grp_w3_0", ("w4", 1): "hb0"}
+        held_behind = {("w3", 1): "ya0"}
 
         def cast_w(name, u, eng, a=0, b=P, slots=2):
             if (name, u) not in grouped:
@@ -199,9 +199,10 @@ def tile_picked_zgatt_sigmoid_po_kernel(tc, x_words, x_scales, w1, w2, w3, w4, o
         load_scales()
         load_w("w1", 1, 4)
         load_x(0, T)
-        for name in ("w2", "w3", "w4"):
+        for name in ("w2", "w3"):
             load_w(name, c1=K // 2)
             load_w(name, c0=K // 2)
+        load_w("w4")
         gather_s("offs")
         gather_s("dst")
         cast_w("w1", 1, "S")
@@ -229,25 +230,24 @@ def tile_picked_zgatt_sigmoid_po_kernel(tc, x_words, x_scales, w1, w2, w3, w4, o
         fifth(1)
         fifth(2)
         cast_w("w3", 0, "V", 64, P)
-        quant_w("w3", 0)
-        cast_w("w3", 1, "G")
         leaky(0)
         for name in ("w1", "w2"):
             for t in range(4):
                 y_pass(3, name, t)
+        cast_w("w3", 1, "G", 64, P)
+        cast_w("w3", 1, "S", 0, 64)
+        quant_w("w3", 0)
         leaky(1)
         leaky(2)
-        cast_w("w4", 0, "S", 0, 64)
         quant_h(0, 2)
         mm_e(0)
         quant_w("w3", 1)
         mm_e(1)
+        cast_w("w4", 0, "V", 0, 64)
         fifth(3)
-        cast_w("w4", 1, "G", 0, 40)
         cast_w("w4", 0, "S", 64, P)
+        cast_w("w4", 1, "S")
         leaky(3)
-        cast_w("w4", 1, "S", 40, 88)
-        cast_w("w4", 1, "V", 88, P)
         quant_w("w4", 0)
         mm_v(0)
         quant_h(2, 4)

@@ -78,7 +78,7 @@ def tile_picked_zgatt_sigmoid_po_kernel(tc, x_words, x_scales, w1, w2, w3, w4, o
             else:
                 nc.gpsimd.tensor_scalar(out, in_, 1.0, 0.0, ALU.mult, ALU.add)
 
-        held_behind = {("w3", 1): "ya0"}
+        held_behind = {("w4", 0): "ya0"}
 
         def cast_w(name, u, eng, a=0, b=P, slots=2):
             if (name, u) not in grouped:
@@ -164,11 +164,12 @@ def tile_picked_zgatt_sigmoid_po_kernel(tc, x_words, x_scales, w1, w2, w3, w4, o
             for t in range(t0, t1):
                 mm(vb[i][:, t - t0, :], t, "w4", words("offs", a // CH, 2), gs["offs"][:, a:b], True, True)
 
-        def mul(i, lo=0, hi=HALF):
+        def mul(i, lo=0, hi=HALF, s0=0, s1=2):
             t0, t1, a, b = pieces[i]
-            nc.vector.tensor_tensor(of[i][:, t0:t1, lo:hi], vb[i][:, :, lo:hi], es[i][:, :, lo:hi], ALU.mult)
+            mine = slice(t0 + s0, t0 + s1)
+            nc.vector.tensor_tensor(of[i][:, mine, lo:hi], vb[i][:, s0:s1, lo:hi], es[i][:, s0:s1, lo:hi], ALU.mult)
             if hi == HALF:
-                nc.sync.dma_start(out_v[:, t0:t1, a:b], of[i][:, t0:t1, :])
+                nc.sync.dma_start(out_v[:, mine, a:b], of[i][:, mine, :])
 
         def cast_o(h, a, b, eng):
             if eng == "G":
@@ -199,10 +200,9 @@ def tile_picked_zgatt_sigmoid_po_kernel(tc, x_words, x_scales, w1, w2, w3, w4, o
         load_scales()
         load_w("w1", 1, 4)
         load_x(0, T)
-        for name in ("w2", "w3"):
+        for name in ("w2", "w3", "w4"):
             load_w(name, c1=K // 2)
             load_w(name, c0=K // 2)
-        load_w("w4")
         gather_s("offs")
         gather_s("dst")
         cast_w("w1", 1, "S")
@@ -226,6 +226,7 @@ def tile_picked_zgatt_sigmoid_po_kernel(tc, x_words, x_scales, w1, w2, w3, w4, o
             for t in (0, 1, 2, 3) if c == 0 else (3, 2, 1, 0):
                 y_pass(c, "w2", t)
         cast_w("w3", 0, "S", 0, 64)
+        cast_w("w3", 1, "V", 0, 64)
         fifth(0)
         fifth(1)
         fifth(2)
@@ -234,8 +235,8 @@ def tile_picked_zgatt_sigmoid_po_kernel(tc, x_words, x_scales, w1, w2, w3, w4, o
         for name in ("w1", "w2"):
             for t in range(4):
                 y_pass(3, name, t)
-        cast_w("w3", 1, "G", 64, P)
-        cast_w("w3", 1, "S", 0, 64)
+        cast_w("w4", 0, "G", 0, 64)
+        cast_w("w3", 1, "S", 64, P)
         quant_w("w3", 0)
         leaky(1)
         leaky(2)
@@ -243,10 +244,10 @@ def tile_picked_zgatt_sigmoid_po_kernel(tc, x_words, x_scales, w1, w2, w3, w4, o
         mm_e(0)
         quant_w("w3", 1)
         mm_e(1)
-        cast_w("w4", 0, "V", 0, 64)
         fifth(3)
         cast_w("w4", 0, "S", 64, P)
-        cast_w("w4", 1, "S")
+        cast_w("w4", 1, "V", 0, 48)
+        cast_w("w4", 1, "S", 48, P)
         leaky(3)
         quant_w("w4", 0)
         mm_v(0)
@@ -259,18 +260,19 @@ def tile_picked_zgatt_sigmoid_po_kernel(tc, x_words, x_scales, w1, w2, w3, w4, o
         mm_v(3)
         for c in range(4):
             sig(c)
-        mul(0)
+        mul(0, s1=1)
+        mul(0, s0=1)
         mul(1)
         cast_o(0, 0, HALF, "S")
         mul(2)
         mul(3, 0, CH)
         mul(3, CH, HALF)
         cast_o(1, 0, CH, "V")
+        quant_o(0, 2)
+        store_w(0, 2)
         cast_o(1, CH, CH + 64, "V")
         cast_o(1, CH + 64, HALF, "S")
         quant_o(2, 3)
-        quant_o(0, 2)
-        store_w(0, 2)
         quant_o(3, 4)
         store_w(2, 4)
         store_scales()

from contextlib import ExitStack

import concourse.mybir as mybir

F32 = mybir.dt.float32
BF16 = mybir.dt.bfloat16
I32 = mybir.dt.int32
U32 = mybir.dt.uint32
U16 = mybir.dt.uint16
U8 = mybir.dt.uint8
FP8X4 = mybir.dt.float8_e4m3fn_x4
ACT = mybir.ActivationFunctionType
ALU = mybir.AluOpType

P = 128
K = 512
T = 2048
S = 512
CH = 128
HALF = S // 2
FLOPS = 4 * 2 * 512 * 512 * 512


def tile_picked_zgatt_sigmoid_po_kernel(tc, x_words, x_scales, w1, w2, w3, w4, offs, dst, out_0, out_1, out_2):
    nc = tc.nc
    with ExitStack() as ctx:
        keep = ctx.enter_context(tc.tile_pool(name="keep", bufs=1))
        psum = ctx.enter_context(tc.psum_pool(name="psum", bufs=1))

        lists = {"offs": keep.tile([P, S // 16], U16, name="offs_t"), "dst": keep.tile([P, S // 16], U16, name="dst_t")}
        xw = keep.tile([P, T], I32, name="xw", align_bytes=64)
        xs = keep.tile([P, T], U8, name="xs", align_bytes=64)
        warm = keep.tile([P, 8], F32, name="warm")
        warm2 = keep.tile([P, 8], F32, name="warm2")
        xw_hbm = x_words[0].rearrange("p n t -> p (n t)").bitcast(I32)
        weights = {"w1": w1, "w2": w2, "w3": w3, "w4": w4}
        raw, gw, gs, grouped, codes, scales = {}, {}, {}, {}, {}, {}
        hq, hs, hb, yb, ya, eb, es, vb, of, ob = {}, {}, {}, {}, {}, {}, {}, {}, {}, {}

        def load_lists():
            nc.sync.dma_start(lists["offs"][:], offs)
            nc.sync.dma_start(lists["dst"][:], dst)

        def load_x(a, b):
            nc.sync.dma_start(xw[:, a:b], xw_hbm[:, a:b])

        def load_scales():
            for q in range(4):
                nc.sync.dma_start(xs[32 * q : 32 * q + 4, :].bitcast(I32), x_scales[0, 4 * q : 4 * q + 4, :].bitcast(I32))

        def load_w(name, j0=0, j1=4, c0=0, c1=K):
            if (name, 0) not in raw:
                raw[name, 0] = keep.tile([P, 4, K], F32, name="raw_%s" % name, align_bytes=64)
            nc.sync.dma_start(raw[name, 0][:, j0:j1, c0:c1], weights[name].rearrange("(p j) c -> p j c", j=4)[:, j0:j1, c0:c1])

        for name in ("offs", "dst"):
            gs[name] = keep.tile([P, S], U8, name="gs_" + name, align_bytes=64)

        def gather_s(name, a=0, b=S):
            nc.vector.tensor_copy(gs[name][:, a:b], xs[:].indirect(lists[name][:, a // 16 : b // 16]))

        def gather_w(name, c0, c1, tag=None):
            mine = "gw_%s%d" % (name, c0)
            tile = keep.tile([P, (c1 - c0) * CH], U32, name=mine, tag=tag or mine, align_bytes=64)
            nc.vector.tensor_copy(tile[:], xw[:].bitcast(U32).indirect(lists[name][:, c0 * CH // 16 : c1 * CH // 16]))
            for c in range(c0, c1):
                gw[name, c] = (tile, c0)

        def words(name, c, n=1):
            tile, c0 = gw[name, c]
            return tile[:, (c - c0) * CH : (c - c0 + n) * CH]

        def copy_on(eng, out, in_):
            if eng == "V":
                nc.vector.tensor_copy(out, in_)
            elif eng == "S":
                nc.scalar.copy(out, in_)
            else:
                nc.gpsimd.tensor_scalar(out, in_, 1.0, 0.0, ALU.mult, ALU.add)

        held_behind = {("w4", 0): "ya0"}

        def cast_w(name, u, eng, a=0, b=P, slots=2):
            if (name, u) not in grouped:
                grouped[name, u] = keep.tile([P, slots, P, 4], BF16, name="grp_%s_%d" % (name, u), tag=held_behind.get((name, u), "grp_%s_%d" % (name, u)), align_bytes=64)
            mine = slice(slots * u, slots * (u + 1))
            if eng == "G":
                src = raw[name, 0][:].rearrange("p j (m t) -> p m t j", t=4)[:, a:b, mine, :]
                copy_on(eng, grouped[name, u][:, :, a:b, :].rearrange("p t m j -> p m t j"), src)
            else:
                src = raw[name, 0][:].rearrange("p j (m t) -> p m j t", t=4)[:, a:b, :, mine]
                copy_on(eng, grouped[name, u][:, :, a:b, :].rearrange("p t m j -> p m j t"), src)

        def quant_w(name, u, slots=2):
            if name not in codes:
                codes[name] = keep.tile([P, K], U32, name="codes_" + name, align_bytes=64)
                scales[name] = keep.tile([P, K], U8, name="scales_" + name, align_bytes=64)
            cols = slice(slots * P * u, slots * P * (u + 1))
            nc.vector.quantize_mx(out=codes[name][:, cols].bitcast(FP8X4), scales=scales[name][:, cols],
                                  in_=grouped[name, u][:].rearrange("p t m j -> p (t m j)"))

        def mm(acc, t, name, rw, rs, start, stop):
            cols = slice(t * P, (t + 1) * P)
            nc.tensor.matmul_mx(out=acc, lhsT=codes[name][:, cols].bitcast(FP8X4),
                                lhsT_scale=scales[name][:, cols],
                                rhs=rw.bitcast(FP8X4), rhs_scale=rs, start=start, stop=stop)

        done = {c: 0 for c in range(4)}

        def y_pass(c, name, t):
            cols = slice(c * CH, (c + 1) * CH)
            if c not in yb:
                yb[c] = psum.tile([P, 4, CH], F32, name="ybank%d" % c, tag="a%d" % (c % 3))
            lst = "offs" if name == "w1" else "dst"
            mm(yb[c][:, t, :], t, name, words(lst, c), gs[lst][:, cols], done[c] == 0, done[c] == 7)
            done[c] = done[c] + 1

        def fifth(c):
            ya[c] = keep.tile([P, CH, 4], F32, name="ya%d" % c, tag="ya%d" % c, align_bytes=64)
            nc.scalar.activation(ya[c][:], yb[c][:].rearrange("p t j -> p j t"), ACT.Copy, scale=0.2)

        for h in range(2):
            ob[h] = keep.tile([P, HALF, 4], BF16, name="ob%d" % h, align_bytes=64)
        hq = keep.tile([P, S], U32, name="hq", align_bytes=64)
        hs = keep.tile([P, S], U8, name="hs", align_bytes=64)
        ow = keep.tile([P, S], U32, name="ow", align_bytes=64)
        osc = keep.tile([P, S], U8, name="osc", align_bytes=64)
        out_v = out_0.rearrange("(p t) j -> p t j", t=4)
        out_w = out_1[0].rearrange("p n t -> p (n t)").bitcast(I32)

        def part(c0, c1):
            return slice((c0 % 2) * CH, (c0 % 2 + c1 - c0) * CH)

        def leaky(c):
            if c % 2 == 0:
                hb[c // 2] = keep.tile([P, HALF, 4], BF16, name="hb%d" % (c // 2), tag="hb%d" % (c // 2), align_bytes=64)
            nc.vector.tensor_tensor(hb[c // 2][:, part(c, c + 1), :], yb[c][:].rearrange("p t j -> p j t"), ya[c][:], ALU.max)

        def quant_h(c0, c1):
            cols = slice(c0 * CH, c1 * CH)
            nc.vector.quantize_mx(out=hq[:, cols].bitcast(FP8X4), scales=hs[:, cols],
                                  in_=hb[c0 // 2][:, part(c0, c1), :].rearrange("p j t -> p (j t)"))

        pieces = [(0, 2, 0, HALF), (2, 4, 0, HALF), (0, 2, HALF, S), (2, 4, HALF, S)]
        of[0] = keep.tile([P, 4, HALF], F32, name="o01", align_bytes=64)
        of[1] = of[0]
        of[2] = keep.tile([P, 4, HALF], F32, name="o23", align_bytes=64)
        of[3] = of[2]

        def mm_e(i):
            t0, t1, a, b = pieces[i]
            eb[i] = psum.tile([P, t1 - t0, b - a], F32, name="ebank%d" % i, tag="b%d" % i)
            for t in range(t0, t1):
                mm(eb[i][:, t - t0, :], t, "w3", hq[:, a:b], hs[:, a:b], True, True)

        def sig(i):
            t0, t1, a, b = pieces[i]
            es[i] = keep.tile([P, t1 - t0, b - a], F32, name="es%d" % i)
            nc.scalar.activation(es[i][:], eb[i][:], ACT.Sigmoid)

        def mm_v(i):
            t0, t1, a, b = pieces[i]
            vb[i] = psum.tile([P, t1 - t0, b - a], F32, name="vbank%d" % i, tag=("a3", "a1", "a2", "a0")[i])
            for t in range(t0, t1):
                mm(vb[i][:, t - t0, :], t, "w4", words("offs", a // CH, 2), gs["offs"][:, a:b], True, True)

        def mul(i, lo=0, hi=HALF, s0=0, s1=2):
            t0, t1, a, b = pieces[i]
            mine = slice(t0 + s0, t0 + s1)
            nc.vector.tensor_tensor(of[i][:, mine, lo:hi], vb[i][:, s0:s1, lo:hi], es[i][:, s0:s1, lo:hi], ALU.mult)
            if hi == HALF:
                nc.sync.dma_start(out_v[:, mine, a:b], of[i][:, mine, :])

        def cast_o(h, a, b, eng):
            if eng == "G":
                copy_on(eng, ob[h][:, a:b, :], of[2 * h][:, :, a:b].rearrange("p t j -> p j t"))
                return
            copy_on(eng, ob[h][:, a:b, :].rearrange("p (c i) t -> p c t i", i=4),
                    of[2 * h][:, :, a:b].rearrange("p t (c i) -> p c t i", i=4))

        def quant_o(c0, c1):
            cols = slice(c0 * CH, c1 * CH)
            nc.vector.quantize_mx(out=ow[:, cols].bitcast(FP8X4), scales=osc[:, cols],
                                  in_=ob[c0 // 2][:, part(c0, c1), :].rearrange("p j t -> p (j t)"))

        def store_w(c0, c1):
            cols = slice(c0 * CH, c1 * CH)
            nc.sync.dma_start(out_w[:, cols], ow[:, cols].bitcast(I32))

        def store_scales():
            for q in range(4):
                eng = nc.scalar if q % 2 == 0 else nc.sync
                eng.dma_start(out_2[0, 4 * q : 4 * q + 4, :].bitcast(I32), osc[32 * q : 32 * q + 4, :].bitcast(I32))

        nc.vector.memset(xs[:].bitcast(I32), 0)
        nc.vector.memset(warm[:], 0.0)
        nc.scalar.activation(warm2[:], warm[:], ACT.Sigmoid)
        load_lists()
        load_w("w1", 0, 1)
        load_scales()
        load_w("w1", 1, 4)
        load_x(0, T)
        for name in ("w2", "w3", "w4"):
            load_w(name, c1=K // 2)
            load_w(name, c0=K // 2)
        gather_s("offs")
        gather_s("dst")
        cast_w("w1", 1, "S")
        cast_w("w1", 0, "V")
        quant_w("w1", 0)
        quant_w("w1", 1)
        gather_w("offs", 0, 2)
        gather_w("offs", 2, 4)
        gather_w("dst", 0, 2)
        for c, t in [(c, t) for t in range(4) for c in (0, 1)] + [(2, t) for t in range(4)]:
            y_pass(c, "w1", t)
        cast_w("w2", 0, "S", 0, 64)
        cast_w("w2", 1, "S", 0, 64)
        cast_w("w2", 0, "V", 64, P)
        cast_w("w2", 1, "V", 64, 80)
        cast_w("w2", 1, "S", 80, P)
        quant_w("w2", 0)
        quant_w("w2", 1)
        gather_w("dst", 2, 4, "grp_w2_1")
        for c in range(3):
            for t in (0, 1, 2, 3) if c == 0 else (3, 2, 1, 0):
                y_pass(c, "w2", t)
        cast_w("w3", 0, "S", 0, 64)
        cast_w("w3", 1, "V", 0, 64)
        fifth(0)
        fifth(1)
        fifth(2)
        cast_w("w3", 0, "V", 64, P)
        leaky(0)
        for name in ("w1", "w2"):
            for t in range(4):
                y_pass(3, name, t)
        cast_w("w4", 0, "G", 0, 64)
        cast_w("w3", 1, "S", 64, P)
        quant_w("w3", 0)
        leaky(1)
        leaky(2)
        quant_h(0, 2)
        mm_e(0)
        quant_w("w3", 1)
        mm_e(1)
        fifth(3)
        cast_w("w4", 0, "S", 64, P)
        cast_w("w4", 1, "V", 0, 48)
        cast_w("w4", 1, "S", 48, P)
        leaky(3)
        quant_w("w4", 0)
        mm_v(0)
        quant_h(2, 4)
        mm_e(2)
        quant_w("w4", 1)
        mm_v(1)
        mm_e(3)
        mm_v(2)
        mm_v(3)
        for c in range(4):
            sig(c)
        mul(0, s1=1)
        mul(0, s0=1)
        mul(1)
        cast_o(0, 0, HALF, "S")
        mul(2)
        mul(3, 0, CH)
        mul(3, CH, HALF)
        cast_o(1, 0, CH, "V")
        quant_o(0, 2)
        store_w(0, 2)
        cast_o(1, CH, CH + 64, "V")
        cast_o(1, CH + 64, HALF, "S")
        quant_o(2, 3)
        quant_o(3, 4)
        store_w(2, 4)
        store_scales()
